import numpy as np
import ml_dtypes


def mxq(x, axis, fmt="e4m3"):
    dtype, down = {"e4m3": (ml_dtypes.float8_e4m3fn, 7), "e5m2": (ml_dtypes.float8_e5m2, 14)}[fmt]
    v = np.moveaxis(np.asarray(x, np.float32).astype(ml_dtypes.bfloat16).astype(np.float64), axis, -1)
    blocks = v.reshape(v.shape[:-1] + (-1, 32))
    amax = np.abs(blocks).max(-1, keepdims=True)
    byte = np.maximum(np.where(amax > 0, np.frexp(amax)[1] - 1 + 127, 0) - down, 1)
    scale = np.exp2(byte - 127.0)
    codes = (blocks / scale).astype(np.float32).astype(dtype).astype(np.float64)
    return np.moveaxis((codes * scale).reshape(v.shape), -1, axis)


WIDE = False


def mx_kscale(k):
    if not WIDE:
        return np.ones(k)
    levels = np.array([10, -10, 5, -5, 0])
    if k % 512:
        return np.exp2(np.random.permutation(np.resize(levels, k // 32))).repeat(32)
    a = np.empty((k // 512, 16))
    for p in range(k // 512):
        a[p, :8] = np.random.permutation(np.resize(levels, 8))
        for g in range(8):
            far = levels[np.abs(levels - a[p, g]) >= 10]
            a[p, g + 8] = far[np.random.randint(len(far))]
    return np.exp2(a.ravel()).repeat(32)


def f64(x):
    return np.asarray(x).astype(np.float64)


def striped(idx):
    return np.tile(idx.reshape(-1, 16).T, (8, 1)).astype(np.uint16)


def unstriped(offs):
    return offs[:16].T.reshape(-1).astype(np.int64)


def relu(v):
    return np.maximum(v, 0.0)


K, T, S, V, H, N = 512, 2048, 1024, 512, 512, 256


def setup_inputs():
    n = np.random.standard_normal
    s = mx_kscale(K)[:, None]
    u = mx_kscale(H)
    return {
        "xT": (n((K, T)) * s).astype(np.float32),
        "w1": (n((K, H)) / np.sqrt(K) / s * u).astype(np.float32),
        "w2": (n((H, N)) / np.sqrt(H) / u[:, None]).astype(np.float32),
        "offs": striped(np.random.permutation(T)[:S]),
    }


def reference(xT, w1, w2, offs):
    xq = mxq(f64(xT)[:, unstriped(offs)], 0, "e4m3")
    h = relu(mxq(f64(w1), 0, "e4m3").T @ xq)
    z = np.abs(h[:, :V] - h[:, V:2 * V])
    return mxq(f64(w2), 0, "e4m3").T @ mxq(z, 0, "e4m3")

@@ -1,0 +1,213 @@
+from contextlib import ExitStack
+
+import concourse.mybir as mybir
+
+K, T, S, V, H, N = 512, 2048, 1024, 512, 512, 256
+FLOPS = 2 * K * H * S + 2 * H * N * V
+
+F32 = mybir.dt.float32
+BF16 = mybir.dt.bfloat16
+U32 = mybir.dt.uint32
+I32 = mybir.dt.int32
+U16 = mybir.dt.uint16
+U8 = mybir.dt.uint8
+FP8X4 = mybir.dt.float8_e4m3fn_x4
+ACT = mybir.ActivationFunctionType
+ALU = mybir.AluOpType
+
+P = 128
+PACK = 4
+GATHER = 256
+PAIRS = 128
+CHUNKS = ((1024,1024,), (512,512,512,512,))
+ABS_ON_VECTOR = (1, 3,)
+
+
+def tile_picked_siam_abs_e_kernel(tc, xT, w1, w2, offs, out):
+    nc = tc.nc
+    with ExitStack() as ctx:
+        keep = ctx.enter_context(tc.tile_pool(name="keep", bufs=1))
+        ring = ctx.enter_context(tc.tile_pool(name="ring", bufs=4))
+        psum = ctx.enter_context(tc.psum_pool(name="psum", bufs=3))
+        psum_out = ctx.enter_context(tc.psum_pool(name="psum_out", bufs=2))
+
+        offsets = keep.tile([P, S // 16], U16, name="offsets")
+
+        x_rows = xT.rearrange("(p j) c -> p j c", j=PACK)
+        raw = {}
+        for u in range(2):
+            c0 = 0
+            for width in CHUNKS[u]:
+                t = keep.tile([P, 2, width], F32, name="x_raw_%d_%d" % (u, c0))
+                nc.sync.dma_start(out=t[:], in_=x_rows[:, 2 * u : 2 * u + 2, c0 : c0 + width])
+                raw[u, c0] = t
+                c0 = c0 + width
+            if u == 0:
+                nc.sync.dma_start(offsets[:], offs)
+
+        w1_rows = w1.rearrange("(p j) c -> p j c", j=PACK)
+        w1_raw = []
+        for h in range(2):
+            t = keep.tile([P, PACK, H // 2], F32, name="w1_raw_%d" % h)
+            nc.sync.dma_start(out=t[:], in_=w1_rows[:, :, h * (H // 2) : (h + 1) * (H // 2)])
+            w1_raw.append(t)
+        w2_raw = keep.tile([P, PACK, N], F32, name="w2_raw")
+        nc.sync.dma_start(out=w2_raw[:], in_=w2.rearrange("(p j) c -> p j c", j=PACK))
+
+        windows = [keep.tile([P, T], U32, name="window_%d" % u) for u in range(2)]
+        picked = [keep.tile([P, GATHER, 2], U32, name="picked_%d" % g, align_bytes=64) for g in range(S // GATHER)]
+        x_codes = [keep.tile([P, GATHER], U32, name="x_codes_%d" % g, align_bytes=64) for g in range(S // GATHER)]
+        x_scales = [keep.tile([P, GATHER], U8, name="x_scales_%d" % g, align_bytes=64) for g in range(S // GATHER)]
+
+        def pair_up(engine, u, c0, a, b):
+            dst = windows[u][:, c0 + a : c0 + b].bitcast(BF16).rearrange("p (n e) -> p n e", e=2)
+            src = raw[u, c0][:, :, a:b].rearrange("p e n -> p n e")
+            if engine == "vector":
+                nc.vector.tensor_copy(out=dst, in_=src)
+            else:
+                nc.scalar.activation(out=dst, in_=src, func=ACT.Copy)
+
+        shared = keep.tile([P, 2048], U32, name="shared", align_bytes=64)
+
+        def gather(u, g):
+            cols = slice(g * GATHER // 16, (g + 1) * GATHER // 16)
+            if g % 2 == 0:
+                dst = picked[g][:, :, u]
+            else:
+                at = 1024 * u + GATHER * (g // 2)
+                dst = shared[:, at : at + GATHER]
+            nc.vector.tensor_copy(out=dst, in_=windows[u][:].indirect(offsets[:, cols]))
+
+        def weave(g):
+            at = GATHER * (g // 2)
+            src = shared[:].bitcast(I32).rearrange("p (u n) -> p n u", u=2)[:, at : at + GATHER, :]
+            nc.vector.tensor_copy(out=picked[g][:].bitcast(I32), in_=src)
+
+        def quantize_x(g):
+            nc.vector.quantize_mx(
+                out=x_codes[g][:].bitcast(FP8X4),
+                scales=x_scales[g][:],
+                in_=picked[g][:].rearrange("p n u -> p (n u)").bitcast(BF16),
+            )
+
+        order = (0, 2, 1, 3)
+        for u in range(2):
+            c0 = 0
+            for i, width in enumerate(CHUNKS[u]):
+                if i == len(CHUNKS[u]) - 1:
+                    cut = (width * 5 // 8)
+                    pair_up("vector", u, c0, 0, cut)
+                    pair_up("scalar", u, c0, cut, width)
+                else:
+                    pair_up("vector" if u == 0 else "scalar", u, c0, 0, width)
+                c0 = c0 + width
+            if u == 0:
+                for g in order:
+                    gather(0, g)
+
+        w1_woven = shared[:, 512:1536].bitcast(BF16).rearrange("p (t m j) -> p t m j", t=PACK, j=PACK)
+        w1_codes = [keep.tile([P, P], U32, name="w1_codes_%d" % t, align_bytes=64) for t in range(PACK)]
+        w1_scales = [keep.tile([P, P], U8, name="w1_scales_%d" % t, align_bytes=64) for t in range(PACK)]
+        w2_woven = keep.tile([P, N, PACK], BF16, name="w2_woven", align_bytes=64)
+        w2_codes = keep.tile([P, N], U32, name="w2_codes", align_bytes=64)
+        w2_scales = keep.tile([P, N], U8, name="w2_scales", align_bytes=64)
+
+        gather(1, 0)
+        gather(1, 2)
+        quantize_x(0)
+        quantize_x(2)
+
+        def weave_w1(engine, h, a, b):
+            dst = w1_woven[:, :, h * (P // 2) + a : h * (P // 2) + b, :].rearrange("p t m j -> p m j t")
+            src = w1_raw[h][:].rearrange("p j (m t) -> p m j t", t=PACK)[:, a:b, :, :]
+            if engine == "vector":
+                nc.vector.tensor_copy(out=dst, in_=src)
+            else:
+                nc.scalar.activation(out=dst, in_=src, func=ACT.Copy)
+
+        weave_w1("scalar", 0, 0, P // 2)
+        weave_w1("scalar", 1, 0, 40)
+        weave_w1("vector", 1, 40, P // 2)
+        for t in range(PACK):
+            nc.vector.quantize_mx(
+                out=w1_codes[t][:].bitcast(FP8X4),
+                scales=w1_scales[t][:],
+                in_=w1_woven[:, t, :, :].rearrange("p m j -> p (m j)"),
+            )
+        gather(1, 1)
+        gather(1, 3)
+        weave(1)
+        weave(3)
+        quantize_x(1)
+        quantize_x(3)
+
+        nc.scalar.activation(
+            out=w2_woven[:].rearrange("p (c i) j -> p c j i", i=4),
+            in_=w2_raw[:].rearrange("p j (c i) -> p c j i", i=4),
+            func=ACT.Copy,
+        )
+        nc.vector.quantize_mx(
+            out=w2_codes[:].bitcast(FP8X4),
+            scales=w2_scales[:],
+            in_=w2_woven[:].rearrange("p c j -> p (c j)"),
+        )
+
+        out_rows = out.rearrange("(r p) v -> p r v", p=P)
+
+        def layer_one(g, cols, bank):
+            for t in range(PACK):
+                nc.tensor.matmul_mx(
+                    out=bank[:, t, :],
+                    lhsT=w1_codes[t][:].bitcast(FP8X4),
+                    lhsT_scale=w1_scales[t][:],
+                    rhs=x_codes[g][:, cols].bitcast(FP8X4),
+                    rhs_scale=x_scales[g][:, cols],
+                    start=True,
+                    stop=True,
+                )
+
+        for c in range(V // PAIRS):
+            g = c * PAIRS // GATHER
+            cols = slice(c * PAIRS % GATHER, c * PAIRS % GATHER + PAIRS)
+            second = psum.tile([P, PACK, PAIRS], F32, name="second")
+            first = psum.tile([P, PACK, PAIRS], F32, name="first")
+            layer_one(g + V // GATHER, cols, second)
+            layer_one(g, cols, first)
+
+            relu_second = ring.tile([P, PAIRS, PACK], F32, name="relu_second")
+            nc.scalar.activation(out=relu_second[:], in_=second[:].rearrange("p t n -> p n t"), func=ACT.Relu)
+            diff = ring.tile([P, PAIRS, PACK], BF16, name="diff")
+            nc.vector.scalar_tensor_tensor(
+                out=diff[:],
+                in0=first[:].rearrange("p t n -> p n t"),
+                scalar=0.0,
+                in1=relu_second[:],
+                op0=ALU.max,
+                op1=ALU.subtract,
+            )
+            z = ring.tile([P, PAIRS, PACK], BF16, name="z", align_bytes=64)
+            if c in ABS_ON_VECTOR:
+                nc.vector.scalar_tensor_tensor(
+                    out=z[:], in0=diff[:], scalar=-1.0, in1=diff[:], op0=ALU.mult, op1=ALU.max
+                )
+            else:
+                nc.scalar.activation(out=z[:], in_=diff[:], func=ACT.Abs)
+            z_codes = ring.tile([P, PAIRS], U32, name="z_codes", align_bytes=64)
+            z_scales = ring.tile([P, PAIRS], U8, name="z_scales", align_bytes=64)
+            nc.vector.quantize_mx(
+                out=z_codes[:].bitcast(FP8X4), scales=z_scales[:], in_=z[:].rearrange("p n t -> p (n t)")
+            )
+            acc = psum_out.tile([P, N // P, PAIRS], F32, name="acc")
+            for r in range(N // P):
+                nc.tensor.matmul_mx(
+                    out=acc[:, r, :],
+                    lhsT=w2_codes[:, r * P : (r + 1) * P].bitcast(FP8X4),
+                    lhsT_scale=w2_scales[:, r * P : (r + 1) * P],
+                    rhs=z_codes[:].bitcast(FP8X4),
+                    rhs_scale=z_scales[:],
+                    start=True,
+                    stop=True,
+                )
+            result = keep.tile([P, N // P, PAIRS], F32, name="result_%d" % c)
+            nc.scalar.activation(out=result[:], in_=acc[:], func=ACT.Copy)
+            nc.sync.dma_start(out=out_rows[:, :, c * PAIRS : (c + 1) * PAIRS], in_=result[:])

@@ -8,7 +8,6 @@ FLOPS = 2 * K * H * S + 2 * H * N * V
 F32 = mybir.dt.float32
 BF16 = mybir.dt.bfloat16
 U32 = mybir.dt.uint32
-I32 = mybir.dt.int32
 U16 = mybir.dt.uint16
 U8 = mybir.dt.uint8
 FP8X4 = mybir.dt.float8_e4m3fn_x4
@@ -19,8 +18,10 @@ P = 128
 PACK = 4
 GATHER = 256
 PAIRS = 128
-CHUNKS = ((1024,1024,), (512,512,512,512,))
-ABS_ON_VECTOR = (1, 3,)
+W1_PARTS = 2
+CHUNKS = ((1024, 1024), (512, 512, 512, 256, 256))
+COPY_ON_VECTOR = (9,)
+ABS_ON_VECTOR = (1, 3)
 
 
 def tile_picked_siam_abs_e_kernel(tc, xT, w1, w2, offs, out):
@@ -28,11 +29,9 @@ def tile_picked_siam_abs_e_kernel(tc, xT, w1, w2, offs, out):
     with ExitStack() as ctx:
         keep = ctx.enter_context(tc.tile_pool(name="keep", bufs=1))
         ring = ctx.enter_context(tc.tile_pool(name="ring", bufs=4))
-        psum = ctx.enter_context(tc.psum_pool(name="psum", bufs=3))
-        psum_out = ctx.enter_context(tc.psum_pool(name="psum_out", bufs=2))
+        psum = ctx.enter_context(tc.psum_pool(name="psum", bufs=8))
 
         offsets = keep.tile([P, S // 16], U16, name="offsets")
-
         x_rows = xT.rearrange("(p j) c -> p j c", j=PACK)
         raw = {}
         for u in range(2):
@@ -47,17 +46,19 @@ def tile_picked_siam_abs_e_kernel(tc, xT, w1, w2, offs, out):
 
         w1_rows = w1.rearrange("(p j) c -> p j c", j=PACK)
         w1_raw = []
-        for h in range(2):
-            t = keep.tile([P, PACK, H // 2], F32, name="w1_raw_%d" % h)
-            nc.sync.dma_start(out=t[:], in_=w1_rows[:, :, h * (H // 2) : (h + 1) * (H // 2)])
+        for h in range(W1_PARTS):
+            t = keep.tile([P, PACK, H // W1_PARTS], F32, name="w1_raw_%d" % h, align_bytes=64)
+            nc.sync.dma_start(out=t[:], in_=w1_rows[:, :, h * (H // W1_PARTS) : (h + 1) * (H // W1_PARTS)])
             w1_raw.append(t)
         w2_raw = keep.tile([P, PACK, N], F32, name="w2_raw")
         nc.sync.dma_start(out=w2_raw[:], in_=w2.rearrange("(p j) c -> p j c", j=PACK))
 
         windows = [keep.tile([P, T], U32, name="window_%d" % u) for u in range(2)]
-        picked = [keep.tile([P, GATHER, 2], U32, name="picked_%d" % g, align_bytes=64) for g in range(S // GATHER)]
+        picked = {g: keep.tile([P, 2 * GATHER], U32, name="picked_%d" % g, align_bytes=64)[:] for g in (0, 2)}
         x_codes = [keep.tile([P, GATHER], U32, name="x_codes_%d" % g, align_bytes=64) for g in range(S // GATHER)]
         x_scales = [keep.tile([P, GATHER], U8, name="x_scales_%d" % g, align_bytes=64) for g in range(S // GATHER)]
+        w1_woven = keep.tile([P, PACK, P, PACK], BF16, name="w1_woven", align_bytes=64)
+        apart = {g: keep.tile([P, 2, GATHER], U32, name="apart_%d" % g) for g in (1, 3)}
 
         def pair_up(engine, u, c0, a, b):
             dst = windows[u][:, c0 + a : c0 + b].bitcast(BF16).rearrange("p (n e) -> p n e", e=2)
@@ -67,94 +68,73 @@ def tile_picked_siam_abs_e_kernel(tc, xT, w1, w2, offs, out):
             else:
                 nc.scalar.activation(out=dst, in_=src, func=ACT.Copy)
 
-        shared = keep.tile([P, 2048], U32, name="shared", align_bytes=64)
-
         def gather(u, g):
             cols = slice(g * GATHER // 16, (g + 1) * GATHER // 16)
-            if g % 2 == 0:
-                dst = picked[g][:, :, u]
-            else:
-                at = 1024 * u + GATHER * (g // 2)
-                dst = shared[:, at : at + GATHER]
+            dst = apart[g][:, u, :] if g in apart else picked[g].rearrange("p (n u) -> p n u", u=2)[:, :, u]
             nc.vector.tensor_copy(out=dst, in_=windows[u][:].indirect(offsets[:, cols]))
 
         def weave(g):
-            at = GATHER * (g // 2)
-            src = shared[:].bitcast(I32).rearrange("p (u n) -> p n u", u=2)[:, at : at + GATHER, :]
-            nc.vector.tensor_copy(out=picked[g][:].bitcast(I32), in_=src)
+            nc.scalar.copy(out=picked[g].rearrange("p (n u) -> p n u", u=2), in_=apart[g][:].rearrange("p u n -> p n u"))
 
         def quantize_x(g):
             nc.vector.quantize_mx(
                 out=x_codes[g][:].bitcast(FP8X4),
                 scales=x_scales[g][:],
-                in_=picked[g][:].rearrange("p n u -> p (n u)").bitcast(BF16),
+                in_=picked[g].bitcast(BF16),
             )
 
-        order = (0, 2, 1, 3)
         for u in range(2):
             c0 = 0
             for i, width in enumerate(CHUNKS[u]):
-                if i == len(CHUNKS[u]) - 1:
-                    cut = (width * 5 // 8)
+                if u == 0 and i == len(CHUNKS[u]) - 1:
+                    cut = width * 5 // 8
                     pair_up("vector", u, c0, 0, cut)
                     pair_up("scalar", u, c0, cut, width)
                 else:
-                    pair_up("vector" if u == 0 else "scalar", u, c0, 0, width)
+                    pair_up("vector" if u == 0 or i >= 3 else "scalar", u, c0, 0, width)
                 c0 = c0 + width
             if u == 0:
-                for g in order:
+                for g in (2, 0, 3, 1):
                     gather(0, g)
 
-        w1_woven = shared[:, 512:1536].bitcast(BF16).rearrange("p (t m j) -> p t m j", t=PACK, j=PACK)
         w1_codes = [keep.tile([P, P], U32, name="w1_codes_%d" % t, align_bytes=64) for t in range(PACK)]
         w1_scales = [keep.tile([P, P], U8, name="w1_scales_%d" % t, align_bytes=64) for t in range(PACK)]
         w2_woven = keep.tile([P, N, PACK], BF16, name="w2_woven", align_bytes=64)
         w2_codes = keep.tile([P, N], U32, name="w2_codes", align_bytes=64)
         w2_scales = keep.tile([P, N], U8, name="w2_scales", align_bytes=64)
 
-        gather(1, 0)
         gather(1, 2)
-        quantize_x(0)
+        gather(1, 0)
         quantize_x(2)
+        quantize_x(0)
+        gather(1, 3)
+        gather(1, 1)
 
-        def weave_w1(engine, h, a, b):
-            dst = w1_woven[:, :, h * (P // 2) + a : h * (P // 2) + b, :].rearrange("p t m j -> p m j t")
-            src = w1_raw[h][:].rearrange("p j (m t) -> p m j t", t=PACK)[:, a:b, :, :]
-            if engine == "vector":
-                nc.vector.tensor_copy(out=dst, in_=src)
-            else:
-                nc.scalar.activation(out=dst, in_=src, func=ACT.Copy)
-
-        weave_w1("scalar", 0, 0, P // 2)
-        weave_w1("scalar", 1, 0, 40)
-        weave_w1("vector", 1, 40, P // 2)
+        for h in range(W1_PARTS):
+            nc.scalar.activation(
+                out=w1_woven[:, :, h * (P // W1_PARTS) : (h + 1) * (P // W1_PARTS), :].rearrange("p t m j -> p m j t"),
+                in_=w1_raw[h][:].rearrange("p j (m t) -> p m j t", t=PACK),
+                func=ACT.Copy,
+            )
         for t in range(PACK):
             nc.vector.quantize_mx(
                 out=w1_codes[t][:].bitcast(FP8X4),
                 scales=w1_scales[t][:],
                 in_=w1_woven[:, t, :, :].rearrange("p m j -> p (m j)"),
             )
-        gather(1, 1)
-        gather(1, 3)
-        weave(1)
-        weave(3)
-        quantize_x(1)
-        quantize_x(3)
 
-        nc.scalar.activation(
-            out=w2_woven[:].rearrange("p (c i) j -> p c j i", i=4),
-            in_=w2_raw[:].rearrange("p j (c i) -> p c j i", i=4),
-            func=ACT.Copy,
-        )
-        nc.vector.quantize_mx(
-            out=w2_codes[:].bitcast(FP8X4),
-            scales=w2_scales[:],
-            in_=w2_woven[:].rearrange("p c j -> p (c j)"),
-        )
+        late = keep.tile([P, 4 * GATHER], U32, name="late", tag="w1_raw_%d" % (W1_PARTS - 1), align_bytes=64)
+        picked[3] = late[:, 0 : 2 * GATHER]
+        picked[1] = late[:, 2 * GATHER : 4 * GATHER]
+        weave(3)
+        weave(1)
 
         out_rows = out.rearrange("(r p) v -> p r v", p=P)
 
-        def layer_one(g, cols, bank):
+        def layer_one(c, side):
+            g = (side * V + c * PAIRS) // GATHER
+            cols = slice(c * PAIRS % GATHER, c * PAIRS % GATHER + PAIRS)
+            bank = psum.tile([P, PACK, PAIRS], F32, name="bank", tag="bank")
             for t in range(PACK):
                 nc.tensor.matmul_mx(
                     out=bank[:, t, :],
@@ -165,17 +145,14 @@ def tile_picked_siam_abs_e_kernel(tc, xT, w1, w2, offs, out):
                     start=True,
                     stop=True,
                 )
+            return bank
 
-        for c in range(V // PAIRS):
-            g = c * PAIRS // GATHER
-            cols = slice(c * PAIRS % GATHER, c * PAIRS % GATHER + PAIRS)
-            second = psum.tile([P, PACK, PAIRS], F32, name="second")
-            first = psum.tile([P, PACK, PAIRS], F32, name="first")
-            layer_one(g + V // GATHER, cols, second)
-            layer_one(g, cols, first)
-
+        def rectify(second):
             relu_second = ring.tile([P, PAIRS, PACK], F32, name="relu_second")
             nc.scalar.activation(out=relu_second[:], in_=second[:].rearrange("p t n -> p n t"), func=ACT.Relu)
+            return relu_second
+
+        def compare(c, first, relu_second):
             diff = ring.tile([P, PAIRS, PACK], BF16, name="diff")
             nc.vector.scalar_tensor_tensor(
                 out=diff[:],
@@ -192,22 +169,67 @@ def tile_picked_siam_abs_e_kernel(tc, xT, w1, w2, offs, out):
                 )
             else:
                 nc.scalar.activation(out=z[:], in_=diff[:], func=ACT.Abs)
+            return z
+
+        def layer_two(r, z_codes, z_scales, acc):
+            nc.tensor.matmul_mx(
+                out=acc,
+                lhsT=w2_codes[:, r * P : (r + 1) * P].bitcast(FP8X4),
+                lhsT_scale=w2_scales[:, r * P : (r + 1) * P],
+                rhs=z_codes[:].bitcast(FP8X4),
+                rhs_scale=z_scales[:],
+                start=True,
+                stop=True,
+            )
+
+        def project(c, z):
             z_codes = ring.tile([P, PAIRS], U32, name="z_codes", align_bytes=64)
             z_scales = ring.tile([P, PAIRS], U8, name="z_scales", align_bytes=64)
             nc.vector.quantize_mx(
                 out=z_codes[:].bitcast(FP8X4), scales=z_scales[:], in_=z[:].rearrange("p n t -> p (n t)")
             )
-            acc = psum_out.tile([P, N // P, PAIRS], F32, name="acc")
-            for r in range(N // P):
-                nc.tensor.matmul_mx(
-                    out=acc[:, r, :],
-                    lhsT=w2_codes[:, r * P : (r + 1) * P].bitcast(FP8X4),
-                    lhsT_scale=w2_scales[:, r * P : (r + 1) * P],
-                    rhs=z_codes[:].bitcast(FP8X4),
-                    rhs_scale=z_scales[:],
-                    start=True,
-                    stop=True,
-                )
             result = keep.tile([P, N // P, PAIRS], F32, name="result_%d" % c)
-            nc.scalar.activation(out=result[:], in_=acc[:], func=ACT.Copy)
+            if c == V // PAIRS - 1:
+                for r in range(N // P):
+                    acc = psum.tile([P, PAIRS], F32, name="acc", tag="bank")
+                    layer_two(r, z_codes, z_scales, acc[:])
+                    if r == 0:
+                        nc.scalar.activation(out=result[:, r, :], in_=acc[:], func=ACT.Copy)
+                    else:
+                        nc.vector.tensor_copy(out=result[:, r, :], in_=acc[:])
+            else:
+                acc = psum.tile([P, N // P, PAIRS], F32, name="acc", tag="bank")
+                for r in range(N // P):
+                    layer_two(r, z_codes, z_scales, acc[:, r, :])
+                if c in COPY_ON_VECTOR:
+                    nc.vector.tensor_copy(out=result[:], in_=acc[:])
+                else:
+                    nc.scalar.activation(out=result[:], in_=acc[:], func=ACT.Copy)
             nc.sync.dma_start(out=out_rows[:, :, c * PAIRS : (c + 1) * PAIRS], in_=result[:])
+
+        quantize_x(3)
+        quantize_x(1)
+        banks = {}
+        for c, side in ((0, 1), (0, 0), (1, 1), (1, 0), (2, 1), (3, 1), (2, 0), (3, 0)):
+            banks[c, side] = layer_one(c, side)
+        nc.scalar.activation(
+            out=w2_woven[:, 0:256, :].rearrange("p (c i) j -> p c j i", i=4),
+            in_=w2_raw[:, :, 0:256].rearrange("p j (c i) -> p c j i", i=4),
+            func=ACT.Copy,
+        )
+        nc.vector.quantize_mx(
+            out=w2_codes[:].bitcast(FP8X4),
+            scales=w2_scales[:],
+            in_=w2_woven[:].rearrange("p c j -> p (c j)"),
+        )
+        rect = [rectify(banks[c, 1]) for c in range(2)]
+        z = [compare(0, banks[0, 0], rect[0])]
+        rect.append(rectify(banks[2, 1]))
+        z.append(compare(1, banks[1, 0], rect[1]))
+        rect.append(rectify(banks[3, 1]))
+        project(0, z[0])
+        z.append(compare(2, banks[2, 0], rect[2]))
+        project(1, z[1])
+        z.append(compare(3, banks[3, 0], rect[3]))
+        project(2, z[2])
+        project(3, z[3])

@@ -8,6 +8,7 @@ FLOPS = 2 * K * H * S + 2 * H * N * V
 F32 = mybir.dt.float32
 BF16 = mybir.dt.bfloat16
 U32 = mybir.dt.uint32
+I32 = mybir.dt.int32
 U16 = mybir.dt.uint16
 U8 = mybir.dt.uint8
 FP8X4 = mybir.dt.float8_e4m3fn_x4
@@ -18,17 +19,14 @@ P = 128
 PACK = 4
 GATHER = 256
 PAIRS = 128
-W1_PARTS = 2
+W1_PARTS = 4
 CHUNKS = ((1024, 1024), (512, 512, 512, 256, 256))
-COPY_ON_VECTOR = (9,)
-ABS_ON_VECTOR = (1, 3)
 
 
 def tile_picked_siam_abs_e_kernel(tc, xT, w1, w2, offs, out):
     nc = tc.nc
     with ExitStack() as ctx:
         keep = ctx.enter_context(tc.tile_pool(name="keep", bufs=1))
-        ring = ctx.enter_context(tc.tile_pool(name="ring", bufs=4))
         psum = ctx.enter_context(tc.psum_pool(name="psum", bufs=8))
 
         offsets = keep.tile([P, S // 16], U16, name="offsets")
@@ -54,11 +52,12 @@ def tile_picked_siam_abs_e_kernel(tc, xT, w1, w2, offs, out):
         nc.sync.dma_start(out=w2_raw[:], in_=w2.rearrange("(p j) c -> p j c", j=PACK))
 
         windows = [keep.tile([P, T], U32, name="window_%d" % u) for u in range(2)]
-        picked = {g: keep.tile([P, 2 * GATHER], U32, name="picked_%d" % g, align_bytes=64)[:] for g in (0, 2)}
+        picked = {g: keep.tile([P, GATHER, 2], U32, name="picked_%d" % g, align_bytes=64) for g in (0, 1, 2)}
         x_codes = [keep.tile([P, GATHER], U32, name="x_codes_%d" % g, align_bytes=64) for g in range(S // GATHER)]
         x_scales = [keep.tile([P, GATHER], U8, name="x_scales_%d" % g, align_bytes=64) for g in range(S // GATHER)]
-        w1_woven = keep.tile([P, PACK, P, PACK], BF16, name="w1_woven", align_bytes=64)
-        apart = {g: keep.tile([P, 2, GATHER], U32, name="apart_%d" % g) for g in (1, 3)}
+        shared = keep.tile([P, 2048], U32, name="shared", align_bytes=64)
+        w1_woven = shared[:, 256:1280].bitcast(BF16).rearrange("p (t m j) -> p t m j", t=PACK, j=PACK)
+        apart = keep.tile([P, 2, GATHER], U32, name="apart")
 
         def pair_up(engine, u, c0, a, b):
             dst = windows[u][:, c0 + a : c0 + b].bitcast(BF16).rearrange("p (n e) -> p n e", e=2)
@@ -70,17 +69,19 @@ def tile_picked_siam_abs_e_kernel(tc, xT, w1, w2, offs, out):
 
         def gather(u, g):
             cols = slice(g * GATHER // 16, (g + 1) * GATHER // 16)
-            dst = apart[g][:, u, :] if g in apart else picked[g].rearrange("p (n u) -> p n u", u=2)[:, :, u]
+            if g == 1:
+                dst = shared[:, 1024 * u : 1024 * u + GATHER]
+            elif g == 3:
+                dst = apart[:, u, :]
+            else:
+                dst = picked[g][:, :, u]
             nc.vector.tensor_copy(out=dst, in_=windows[u][:].indirect(offsets[:, cols]))
-
-        def weave(g):
-            nc.scalar.copy(out=picked[g].rearrange("p (n u) -> p n u", u=2), in_=apart[g][:].rearrange("p u n -> p n u"))
 
         def quantize_x(g):
             nc.vector.quantize_mx(
                 out=x_codes[g][:].bitcast(FP8X4),
                 scales=x_scales[g][:],
-                in_=picked[g].bitcast(BF16),
+                in_=picked[g][:].rearrange("p n u -> p (n u)").bitcast(BF16),
             )
 
         for u in range(2):
@@ -108,7 +109,6 @@ def tile_picked_siam_abs_e_kernel(tc, xT, w1, w2, offs, out):
         quantize_x(2)
         quantize_x(0)
         gather(1, 3)
-        gather(1, 1)
 
         for h in range(W1_PARTS):
             nc.scalar.activation(
@@ -122,12 +122,15 @@ def tile_picked_siam_abs_e_kernel(tc, xT, w1, w2, offs, out):
                 scales=w1_scales[t][:],
                 in_=w1_woven[:, t, :, :].rearrange("p m j -> p (m j)"),
             )
-
-        late = keep.tile([P, 4 * GATHER], U32, name="late", tag="w1_raw_%d" % (W1_PARTS - 1), align_bytes=64)
-        picked[3] = late[:, 0 : 2 * GATHER]
-        picked[1] = late[:, 2 * GATHER : 4 * GATHER]
-        weave(3)
-        weave(1)
+        picked[3] = keep.tile([P, GATHER, 2], U32, name="late", tag="w1_raw_%d" % (W1_PARTS - 1), align_bytes=64)
+        nc.scalar.copy(out=picked[3][:], in_=apart[:].rearrange("p u n -> p n u"))
+        gather(1, 1)
+        quantize_x(3)
+        nc.vector.tensor_copy(
+            out=picked[1][:].bitcast(I32),
+            in_=shared[:].bitcast(I32).rearrange("p (u n) -> p n u", u=2)[:, 0:GATHER, :],
+        )
+        quantize_x(1)
 
         out_rows = out.rearrange("(r p) v -> p r v", p=P)
 
@@ -147,29 +150,44 @@ def tile_picked_siam_abs_e_kernel(tc, xT, w1, w2, offs, out):
                 )
             return bank
 
-        def rectify(second):
-            relu_second = ring.tile([P, PAIRS, PACK], F32, name="relu_second")
-            nc.scalar.activation(out=relu_second[:], in_=second[:].rearrange("p t n -> p n t"), func=ACT.Relu)
-            return relu_second
+        banks, rect, diff, z = {}, {}, {}, {}
 
-        def compare(c, first, relu_second):
-            diff = ring.tile([P, PAIRS, PACK], BF16, name="diff")
+        def rectify(c):
+            rect[c] = keep.tile([P, PACK, PAIRS], F32, name="rect_%d" % c)
+            nc.scalar.activation(out=rect[c][:], in_=banks[c, 1][:], func=ACT.Relu)
+
+        def subtract(c):
+            diff[c] = keep.tile([P, PACK, PAIRS], F32, name="diff_%d" % c)
             nc.vector.scalar_tensor_tensor(
-                out=diff[:],
-                in0=first[:].rearrange("p t n -> p n t"),
+                out=diff[c][:],
+                in0=banks[c, 0][:],
                 scalar=0.0,
-                in1=relu_second[:],
+                in1=rect[c][:],
                 op0=ALU.max,
                 op1=ALU.subtract,
             )
-            z = ring.tile([P, PAIRS, PACK], BF16, name="z", align_bytes=64)
-            if c in ABS_ON_VECTOR:
-                nc.vector.scalar_tensor_tensor(
-                    out=z[:], in0=diff[:], scalar=-1.0, in1=diff[:], op0=ALU.mult, op1=ALU.max
-                )
-            else:
-                nc.scalar.activation(out=z[:], in_=diff[:], func=ACT.Abs)
-            return z
+
+        def absolute(c):
+            z[c] = keep.tile([P, PAIRS, PACK], BF16, name="z_%d" % c, align_bytes=64)
+            nc.scalar.activation(
+                out=z[c][:].rearrange("p (c i) t -> p c t i", i=4),
+                in_=diff[c][:].rearrange("p t (c i) -> p c t i", i=4),
+                func=ACT.Abs,
+            )
+
+        def weave_w2():
+            nc.scalar.activation(
+                out=w2_woven[:].rearrange("p (c i) j -> p c j i", i=4),
+                in_=w2_raw[:].rearrange("p j (c i) -> p c j i", i=4),
+                func=ACT.Copy,
+            )
+
+        def quantize_w2():
+            nc.vector.quantize_mx(
+                out=w2_codes[:].bitcast(FP8X4),
+                scales=w2_scales[:],
+                in_=w2_woven[:].rearrange("p c j -> p (c j)"),
+            )
 
         def layer_two(r, z_codes, z_scales, acc):
             nc.tensor.matmul_mx(
@@ -182,11 +200,11 @@ def tile_picked_siam_abs_e_kernel(tc, xT, w1, w2, offs, out):
                 stop=True,
             )
 
-        def project(c, z):
-            z_codes = ring.tile([P, PAIRS], U32, name="z_codes", align_bytes=64)
-            z_scales = ring.tile([P, PAIRS], U8, name="z_scales", align_bytes=64)
+        def project(c):
+            z_codes = keep.tile([P, PAIRS], U32, name="z_codes_%d" % c, align_bytes=64)
+            z_scales = keep.tile([P, PAIRS], U8, name="z_scales_%d" % c, align_bytes=64)
             nc.vector.quantize_mx(
-                out=z_codes[:].bitcast(FP8X4), scales=z_scales[:], in_=z[:].rearrange("p n t -> p (n t)")
+                out=z_codes[:].bitcast(FP8X4), scales=z_scales[:], in_=z[c][:].rearrange("p n t -> p (n t)")
             )
             result = keep.tile([P, N // P, PAIRS], F32, name="result_%d" % c)
             if c == V // PAIRS - 1:
@@ -201,35 +219,26 @@ def tile_picked_siam_abs_e_kernel(tc, xT, w1, w2, offs, out):
                 acc = psum.tile([P, N // P, PAIRS], F32, name="acc", tag="bank")
                 for r in range(N // P):
                     layer_two(r, z_codes, z_scales, acc[:, r, :])
-                if c in COPY_ON_VECTOR:
-                    nc.vector.tensor_copy(out=result[:], in_=acc[:])
-                else:
-                    nc.scalar.activation(out=result[:], in_=acc[:], func=ACT.Copy)
+                nc.scalar.activation(out=result[:], in_=acc[:], func=ACT.Copy)
             nc.sync.dma_start(out=out_rows[:, :, c * PAIRS : (c + 1) * PAIRS], in_=result[:])
 
-        quantize_x(3)
-        quantize_x(1)
-        banks = {}
         for c, side in ((0, 1), (0, 0), (1, 1), (1, 0), (2, 1), (3, 1), (2, 0), (3, 0)):
             banks[c, side] = layer_one(c, side)
-        nc.scalar.activation(
-            out=w2_woven[:, 0:256, :].rearrange("p (c i) j -> p c j i", i=4),
-            in_=w2_raw[:, :, 0:256].rearrange("p j (c i) -> p c j i", i=4),
-            func=ACT.Copy,
-        )
-        nc.vector.quantize_mx(
-            out=w2_codes[:].bitcast(FP8X4),
-            scales=w2_scales[:],
-            in_=w2_woven[:].rearrange("p c j -> p (c j)"),
-        )
-        rect = [rectify(banks[c, 1]) for c in range(2)]
-        z = [compare(0, banks[0, 0], rect[0])]
-        rect.append(rectify(banks[2, 1]))
-        z.append(compare(1, banks[1, 0], rect[1]))
-        rect.append(rectify(banks[3, 1]))
-        project(0, z[0])
-        z.append(compare(2, banks[2, 0], rect[2]))
-        project(1, z[1])
-        z.append(compare(3, banks[3, 0], rect[3]))
-        project(2, z[2])
-        project(3, z[3])
+        rectify(0)
+        rectify(1)
+        weave_w2()
+        subtract(0)
+        subtract(1)
+        rectify(2)
+        rectify(3)
+        absolute(0)
+        absolute(1)
+        subtract(2)
+        quantize_w2()
+        absolute(2)
+        subtract(3)
+        absolute(3)
+        project(0)
+        project(1)
+        project(2)
+        project(3)

@@ -17,228 +17,208 @@ ALU = mybir.AluOpType
 
 P = 128
 PACK = 4
-GATHER = 256
-PAIRS = 128
-W1_PARTS = 4
-CHUNKS = ((1024, 1024), (512, 512, 512, 256, 256))
+LIST_ROWS = 16
+GROUP = 256
+CHUNK = 128
+CHUNKS = V // CHUNK
+BANKS = 8
+
+FIRST_EARLY, FIRST_LATE, SECOND_EARLY, SECOND_LATE = range(4)
+FIRST, SECOND = 0, 1
+
+X_LOADS = ((1024, 1024), (512, 512, 512, 256, 256))
+X_ON_VECTOR = ((1024, 640), (0, 0, 0, 256, 256))
+W1_LOADS = (32, 48, 48)
+W2_ON_SCALAR = 160
 
 
 def tile_picked_siam_abs_e_kernel(tc, xT, w1, w2, offs, out):
     nc = tc.nc
+
+    def round_copy(on_vector, dst, src):
+        if on_vector:
+            nc.vector.tensor_copy(out=dst, in_=src)
+        else:
+            nc.scalar.activation(out=dst, in_=src, func=ACT.Copy)
+
+    def quantize(codes, scales, values):
+        nc.vector.quantize_mx(out=codes[:].bitcast(FP8X4), scales=scales[:], in_=values)
+
+    def multiply(acc, w_codes, w_scales, codes, scales):
+        nc.tensor.matmul_mx(
+            out=acc,
+            lhsT=w_codes.bitcast(FP8X4),
+            lhsT_scale=w_scales,
+            rhs=codes.bitcast(FP8X4),
+            rhs_scale=scales,
+            start=True,
+            stop=True,
+        )
+
     with ExitStack() as ctx:
         keep = ctx.enter_context(tc.tile_pool(name="keep", bufs=1))
-        psum = ctx.enter_context(tc.psum_pool(name="psum", bufs=8))
+        psum = ctx.enter_context(tc.psum_pool(name="psum", bufs=BANKS))
 
-        offsets = keep.tile([P, S // 16], U16, name="offsets")
+        def mx_tiles(name, width):
+            codes = keep.tile([P, width], U32, name=name + "_codes", align_bytes=64)
+            scales = keep.tile([P, width], U8, name=name + "_scales", align_bytes=64)
+            return codes, scales
+
+        offsets = keep.tile([P, S // LIST_ROWS], U16, name="offsets")
         x_rows = xT.rearrange("(p j) c -> p j c", j=PACK)
-        raw = {}
+        x_raw = {}
         for u in range(2):
-            c0 = 0
-            for width in CHUNKS[u]:
-                t = keep.tile([P, 2, width], F32, name="x_raw_%d_%d" % (u, c0))
-                nc.sync.dma_start(out=t[:], in_=x_rows[:, 2 * u : 2 * u + 2, c0 : c0 + width])
-                raw[u, c0] = t
-                c0 = c0 + width
+            for i, width in enumerate(X_LOADS[u]):
+                start = sum(X_LOADS[u][:i])
+                x_raw[u, i] = keep.tile([P, 2, width], F32, name="x_raw_%d_%d" % (u, i))
+                nc.sync.dma_start(out=x_raw[u, i][:], in_=x_rows[:, 2 * u : 2 * u + 2, start : start + width])
             if u == 0:
                 nc.sync.dma_start(offsets[:], offs)
 
         w1_rows = w1.rearrange("(p j) c -> p j c", j=PACK)
         w1_raw = []
-        for h in range(W1_PARTS):
-            t = keep.tile([P, PACK, H // W1_PARTS], F32, name="w1_raw_%d" % h, align_bytes=64)
-            nc.sync.dma_start(out=t[:], in_=w1_rows[:, :, h * (H // W1_PARTS) : (h + 1) * (H // W1_PARTS)])
-            w1_raw.append(t)
+        for h, width in enumerate(W1_LOADS):
+            start = PACK * sum(W1_LOADS[:h])
+            part = keep.tile([P, PACK, PACK * width], F32, name="w1_raw_%d" % h, align_bytes=64)
+            nc.sync.dma_start(out=part[:], in_=w1_rows[:, :, start : start + PACK * width])
+            w1_raw.append(part)
         w2_raw = keep.tile([P, PACK, N], F32, name="w2_raw")
         nc.sync.dma_start(out=w2_raw[:], in_=w2.rearrange("(p j) c -> p j c", j=PACK))
 
         windows = [keep.tile([P, T], U32, name="window_%d" % u) for u in range(2)]
-        picked = {g: keep.tile([P, GATHER, 2], U32, name="picked_%d" % g, align_bytes=64) for g in (0, 1, 2)}
-        x_codes = [keep.tile([P, GATHER], U32, name="x_codes_%d" % g, align_bytes=64) for g in range(S // GATHER)]
-        x_scales = [keep.tile([P, GATHER], U8, name="x_scales_%d" % g, align_bytes=64) for g in range(S // GATHER)]
-        shared = keep.tile([P, 2048], U32, name="shared", align_bytes=64)
-        w1_woven = shared[:, 256:1280].bitcast(BF16).rearrange("p (t m j) -> p t m j", t=PACK, j=PACK)
-        apart = keep.tile([P, 2, GATHER], U32, name="apart")
+        x_mx = [mx_tiles("x_%d" % g, GROUP) for g in range(S // GROUP)]
 
-        def pair_up(engine, u, c0, a, b):
-            dst = windows[u][:, c0 + a : c0 + b].bitcast(BF16).rearrange("p (n e) -> p n e", e=2)
-            src = raw[u, c0][:, :, a:b].rearrange("p e n -> p n e")
-            if engine == "vector":
-                nc.vector.tensor_copy(out=dst, in_=src)
-            else:
-                nc.scalar.activation(out=dst, in_=src, func=ACT.Copy)
+        picked = {
+            g: keep.tile([P, GROUP, 2], U32, name="picked_%d" % g, align_bytes=64)
+            for g in (FIRST_EARLY, FIRST_LATE, SECOND_EARLY)
+        }
+        second_late_runs = keep.tile([P, 2, GROUP], U32, name="second_late_runs")
+
+        half = PACK * P * PACK // 2
+        shared = keep.tile([P, 2 * half], U32, name="shared", align_bytes=64)
+        w1_woven = shared[:, GROUP : GROUP + half].bitcast(BF16).rearrange("p (t m j) -> p t m j", t=PACK, j=PACK)
 
         def gather(u, g):
-            cols = slice(g * GATHER // 16, (g + 1) * GATHER // 16)
-            if g == 1:
-                dst = shared[:, 1024 * u : 1024 * u + GATHER]
-            elif g == 3:
-                dst = apart[:, u, :]
+            if g == FIRST_LATE:
+                dst = shared[:, u * half : u * half + GROUP]
+            elif g == SECOND_LATE:
+                dst = second_late_runs[:, u, :]
             else:
                 dst = picked[g][:, :, u]
-            nc.vector.tensor_copy(out=dst, in_=windows[u][:].indirect(offsets[:, cols]))
+            entries = offsets[:, g * GROUP // LIST_ROWS : (g + 1) * GROUP // LIST_ROWS]
+            nc.vector.tensor_copy(out=dst, in_=windows[u][:].indirect(entries))
 
         def quantize_x(g):
-            nc.vector.quantize_mx(
-                out=x_codes[g][:].bitcast(FP8X4),
-                scales=x_scales[g][:],
-                in_=picked[g][:].rearrange("p n u -> p (n u)").bitcast(BF16),
-            )
+            quantize(*x_mx[g], picked[g][:].rearrange("p n u -> p (n u)").bitcast(BF16))
 
         for u in range(2):
-            c0 = 0
-            for i, width in enumerate(CHUNKS[u]):
-                if u == 0 and i == len(CHUNKS[u]) - 1:
-                    cut = width * 5 // 8
-                    pair_up("vector", u, c0, 0, cut)
-                    pair_up("scalar", u, c0, cut, width)
-                else:
-                    pair_up("vector" if u == 0 or i >= 3 else "scalar", u, c0, 0, width)
-                c0 = c0 + width
+            for i, width in enumerate(X_LOADS[u]):
+                start = sum(X_LOADS[u][:i])
+                cut = X_ON_VECTOR[u][i]
+                for on_vector, a, b in ((True, 0, cut), (False, cut, width)):
+                    if a < b:
+                        round_copy(
+                            on_vector,
+                            windows[u][:, start + a : start + b].bitcast(BF16).rearrange("p (n e) -> p n e", e=2),
+                            x_raw[u, i][:, :, a:b].rearrange("p e n -> p n e"),
+                        )
             if u == 0:
-                for g in (2, 0, 3, 1):
+                for g in (SECOND_EARLY, FIRST_EARLY, SECOND_LATE, FIRST_LATE):
                     gather(0, g)
 
-        w1_codes = [keep.tile([P, P], U32, name="w1_codes_%d" % t, align_bytes=64) for t in range(PACK)]
-        w1_scales = [keep.tile([P, P], U8, name="w1_scales_%d" % t, align_bytes=64) for t in range(PACK)]
-        w2_woven = keep.tile([P, N, PACK], BF16, name="w2_woven", align_bytes=64)
-        w2_codes = keep.tile([P, N], U32, name="w2_codes", align_bytes=64)
-        w2_scales = keep.tile([P, N], U8, name="w2_scales", align_bytes=64)
+        gather(1, SECOND_EARLY)
+        gather(1, FIRST_EARLY)
+        quantize_x(SECOND_EARLY)
+        quantize_x(FIRST_EARLY)
+        gather(1, SECOND_LATE)
 
-        gather(1, 2)
-        gather(1, 0)
-        quantize_x(2)
-        quantize_x(0)
-        gather(1, 3)
-
-        for h in range(W1_PARTS):
-            nc.scalar.activation(
-                out=w1_woven[:, :, h * (P // W1_PARTS) : (h + 1) * (P // W1_PARTS), :].rearrange("p t m j -> p m j t"),
-                in_=w1_raw[h][:].rearrange("p j (m t) -> p m j t", t=PACK),
-                func=ACT.Copy,
+        w1_mx = [mx_tiles("w1_%d" % t, P) for t in range(PACK)]
+        for h, width in enumerate(W1_LOADS):
+            start = sum(W1_LOADS[:h])
+            round_copy(
+                False,
+                w1_woven[:, :, start : start + width, :].rearrange("p t m j -> p m j t"),
+                w1_raw[h][:].rearrange("p j (m t) -> p m j t", t=PACK),
             )
         for t in range(PACK):
-            nc.vector.quantize_mx(
-                out=w1_codes[t][:].bitcast(FP8X4),
-                scales=w1_scales[t][:],
-                in_=w1_woven[:, t, :, :].rearrange("p m j -> p (m j)"),
-            )
-        picked[3] = keep.tile([P, GATHER, 2], U32, name="late", tag="w1_raw_%d" % (W1_PARTS - 1), align_bytes=64)
-        nc.scalar.copy(out=picked[3][:], in_=apart[:].rearrange("p u n -> p n u"))
-        gather(1, 1)
-        quantize_x(3)
-        nc.vector.tensor_copy(
-            out=picked[1][:].bitcast(I32),
-            in_=shared[:].bitcast(I32).rearrange("p (u n) -> p n u", u=2)[:, 0:GATHER, :],
+            quantize(*w1_mx[t], w1_woven[:, t, :, :].rearrange("p m j -> p (m j)"))
+
+        picked[SECOND_LATE] = keep.tile(
+            [P, GROUP, 2], U32, name="picked_second_late", tag="w1_raw_%d" % (len(W1_LOADS) - 1), align_bytes=64
         )
-        quantize_x(1)
+        nc.scalar.copy(out=picked[SECOND_LATE][:], in_=second_late_runs[:].rearrange("p u n -> p n u"))
+        gather(1, FIRST_LATE)
+        quantize_x(SECOND_LATE)
+        nc.vector.tensor_copy(
+            out=picked[FIRST_LATE][:].bitcast(I32),
+            in_=shared[:].bitcast(I32).rearrange("p (u n) -> p n u", u=2)[:, 0:GROUP, :],
+        )
+        quantize_x(FIRST_LATE)
 
-        out_rows = out.rearrange("(r p) v -> p r v", p=P)
-
-        def layer_one(c, side):
-            g = (side * V + c * PAIRS) // GATHER
-            cols = slice(c * PAIRS % GATHER, c * PAIRS % GATHER + PAIRS)
-            bank = psum.tile([P, PACK, PAIRS], F32, name="bank", tag="bank")
+        bank = {}
+        early = [(c, side) for c in range(CHUNKS // 2) for side in (SECOND, FIRST)]
+        late = [(c, side) for side in (SECOND, FIRST) for c in range(CHUNKS // 2, CHUNKS)]
+        for c, side in early + late:
+            entry = side * V + c * CHUNK
+            codes, scales = x_mx[entry // GROUP]
+            cols = slice(entry % GROUP, entry % GROUP + CHUNK)
+            bank[c, side] = psum.tile([P, PACK, CHUNK], F32, name="hidden", tag="bank")
             for t in range(PACK):
-                nc.tensor.matmul_mx(
-                    out=bank[:, t, :],
-                    lhsT=w1_codes[t][:].bitcast(FP8X4),
-                    lhsT_scale=w1_scales[t][:],
-                    rhs=x_codes[g][:, cols].bitcast(FP8X4),
-                    rhs_scale=x_scales[g][:, cols],
-                    start=True,
-                    stop=True,
-                )
-            return bank
+                multiply(bank[c, side][:, t, :], w1_mx[t][0][:], w1_mx[t][1][:], codes[:, cols], scales[:, cols])
 
-        banks, rect, diff, z = {}, {}, {}, {}
+        w2_woven = keep.tile([P, N, PACK], BF16, name="w2_woven", align_bytes=64)
+        w2_codes, w2_scales = mx_tiles("w2", N)
+        for on_vector, a, b in ((False, 0, W2_ON_SCALAR), (True, W2_ON_SCALAR, N)):
+            round_copy(
+                on_vector,
+                w2_woven[:, a:b, :].rearrange("p (c i) j -> p c j i", i=4),
+                w2_raw[:, :, a:b].rearrange("p j (c i) -> p c j i", i=4),
+            )
+        quantize(w2_codes, w2_scales, w2_woven[:].rearrange("p c j -> p (c j)"))
 
-        def rectify(c):
-            rect[c] = keep.tile([P, PACK, PAIRS], F32, name="rect_%d" % c)
-            nc.scalar.activation(out=rect[c][:], in_=banks[c, 1][:], func=ACT.Relu)
-
-        def subtract(c):
-            diff[c] = keep.tile([P, PACK, PAIRS], F32, name="diff_%d" % c)
+        relu_second = [keep.tile([P, CHUNK, PACK], F32, name="relu_second_%d" % c) for c in range(CHUNKS)]
+        diff = [keep.tile([P, CHUNK, PACK], BF16, name="diff_%d" % c) for c in range(CHUNKS)]
+        z = [keep.tile([P, CHUNK, PACK], BF16, name="z_%d" % c, align_bytes=64) for c in range(CHUNKS)]
+        for c in range(CHUNKS):
+            nc.scalar.activation(
+                out=relu_second[c][:], in_=bank[c, SECOND][:].rearrange("p t n -> p n t"), func=ACT.Relu
+            )
+        for c in range(CHUNKS):
             nc.vector.scalar_tensor_tensor(
                 out=diff[c][:],
-                in0=banks[c, 0][:],
+                in0=bank[c, FIRST][:].rearrange("p t n -> p n t"),
                 scalar=0.0,
-                in1=rect[c][:],
+                in1=relu_second[c][:],
                 op0=ALU.max,
                 op1=ALU.subtract,
             )
+        for c in range(CHUNKS):
+            cut = CHUNK if c < CHUNKS - 1 else CHUNK // 2
+            nc.scalar.activation(out=z[c][:, 0:cut, :], in_=diff[c][:, 0:cut, :], func=ACT.Abs)
+            if cut < CHUNK:
+                rest = diff[c][:, cut:CHUNK, :]
+                nc.vector.scalar_tensor_tensor(
+                    out=z[c][:, cut:CHUNK, :], in0=rest, scalar=-1.0, in1=rest, op0=ALU.mult, op1=ALU.max
+                )
 
-        def absolute(c):
-            z[c] = keep.tile([P, PAIRS, PACK], BF16, name="z_%d" % c, align_bytes=64)
-            nc.scalar.activation(
-                out=z[c][:].rearrange("p (c i) t -> p c t i", i=4),
-                in_=diff[c][:].rearrange("p t (c i) -> p c t i", i=4),
-                func=ACT.Abs,
-            )
-
-        def weave_w2():
-            nc.scalar.activation(
-                out=w2_woven[:].rearrange("p (c i) j -> p c j i", i=4),
-                in_=w2_raw[:].rearrange("p j (c i) -> p c j i", i=4),
-                func=ACT.Copy,
-            )
-
-        def quantize_w2():
-            nc.vector.quantize_mx(
-                out=w2_codes[:].bitcast(FP8X4),
-                scales=w2_scales[:],
-                in_=w2_woven[:].rearrange("p c j -> p (c j)"),
-            )
-
-        def layer_two(r, z_codes, z_scales, acc):
-            nc.tensor.matmul_mx(
-                out=acc,
-                lhsT=w2_codes[:, r * P : (r + 1) * P].bitcast(FP8X4),
-                lhsT_scale=w2_scales[:, r * P : (r + 1) * P],
-                rhs=z_codes[:].bitcast(FP8X4),
-                rhs_scale=z_scales[:],
-                start=True,
-                stop=True,
-            )
-
-        def project(c):
-            z_codes = keep.tile([P, PAIRS], U32, name="z_codes_%d" % c, align_bytes=64)
-            z_scales = keep.tile([P, PAIRS], U8, name="z_scales_%d" % c, align_bytes=64)
-            nc.vector.quantize_mx(
-                out=z_codes[:].bitcast(FP8X4), scales=z_scales[:], in_=z[c][:].rearrange("p n t -> p (n t)")
-            )
-            result = keep.tile([P, N // P, PAIRS], F32, name="result_%d" % c)
-            if c == V // PAIRS - 1:
+        out_rows = out.rearrange("(r p) v -> p r v", p=P)
+        for c in range(CHUNKS):
+            z_codes, z_scales = mx_tiles("z_%d" % c, CHUNK)
+            quantize(z_codes, z_scales, z[c][:].rearrange("p n t -> p (n t)"))
+            result = keep.tile([P, N // P, CHUNK], F32, name="result_%d" % c)
+            if c < CHUNKS - 1:
+                acc = psum.tile([P, N // P, CHUNK], F32, name="acc", tag="bank")
                 for r in range(N // P):
-                    acc = psum.tile([P, PAIRS], F32, name="acc", tag="bank")
-                    layer_two(r, z_codes, z_scales, acc[:])
+                    rows = slice(r * P, (r + 1) * P)
+                    multiply(acc[:, r, :], w2_codes[:, rows], w2_scales[:, rows], z_codes[:], z_scales[:])
+                nc.scalar.activation(out=result[:], in_=acc[:], func=ACT.Copy)
+            else:
+                for r in range(N // P):
+                    rows = slice(r * P, (r + 1) * P)
+                    acc = psum.tile([P, CHUNK], F32, name="acc", tag="bank")
+                    multiply(acc[:], w2_codes[:, rows], w2_scales[:, rows], z_codes[:], z_scales[:])
                     if r == 0:
                         nc.scalar.activation(out=result[:, r, :], in_=acc[:], func=ACT.Copy)
                     else:
                         nc.vector.tensor_copy(out=result[:, r, :], in_=acc[:])
-            else:
-                acc = psum.tile([P, N // P, PAIRS], F32, name="acc", tag="bank")
-                for r in range(N // P):
-                    layer_two(r, z_codes, z_scales, acc[:, r, :])
-                nc.scalar.activation(out=result[:], in_=acc[:], func=ACT.Copy)
-            nc.sync.dma_start(out=out_rows[:, :, c * PAIRS : (c + 1) * PAIRS], in_=result[:])
-
-        for c, side in ((0, 1), (0, 0), (1, 1), (1, 0), (2, 1), (3, 1), (2, 0), (3, 0)):
-            banks[c, side] = layer_one(c, side)
-        rectify(0)
-        rectify(1)
-        weave_w2()
-        subtract(0)
-        subtract(1)
-        rectify(2)
-        rectify(3)
-        absolute(0)
-        absolute(1)
-        subtract(2)
-        quantize_w2()
-        absolute(2)
-        subtract(3)
-        absolute(3)
-        project(0)
-        project(1)
-        project(2)
-        project(3)
+            nc.sync.dma_start(out=out_rows[:, :, c * CHUNK : (c + 1) * CHUNK], in_=result[:])

from contextlib import ExitStack

import concourse.mybir as mybir

K, T, S, V, H, N = 512, 2048, 1024, 512, 512, 256
FLOPS = 2 * K * H * S + 2 * H * N * V

F32 = mybir.dt.float32
BF16 = mybir.dt.bfloat16
U32 = mybir.dt.uint32
I32 = mybir.dt.int32
U16 = mybir.dt.uint16
U8 = mybir.dt.uint8
FP8X4 = mybir.dt.float8_e4m3fn_x4
ACT = mybir.ActivationFunctionType
ALU = mybir.AluOpType

P = 128
PACK = 4
LIST_ROWS = 16
GROUP = 256
CHUNK = 128
CHUNKS = V // CHUNK
BANKS = 8

FIRST_EARLY, FIRST_LATE, SECOND_EARLY, SECOND_LATE = range(4)
FIRST, SECOND = 0, 1

X_LOADS = ((1024, 1024), (512, 512, 512, 256, 256))
X_ON_VECTOR = ((1024, 640), (0, 0, 0, 256, 256))
W1_LOADS = (32, 48, 48)
W2_ON_SCALAR = 160


def tile_picked_siam_abs_e_kernel(tc, xT, w1, w2, offs, out):
    nc = tc.nc

    def round_copy(on_vector, dst, src):
        if on_vector:
            nc.vector.tensor_copy(out=dst, in_=src)
        else:
            nc.scalar.activation(out=dst, in_=src, func=ACT.Copy)

    def quantize(codes, scales, values):
        nc.vector.quantize_mx(out=codes[:].bitcast(FP8X4), scales=scales[:], in_=values)

    def multiply(acc, w_codes, w_scales, codes, scales):
        nc.tensor.matmul_mx(
            out=acc,
            lhsT=w_codes.bitcast(FP8X4),
            lhsT_scale=w_scales,
            rhs=codes.bitcast(FP8X4),
            rhs_scale=scales,
            start=True,
            stop=True,
        )

    with ExitStack() as ctx:
        keep = ctx.enter_context(tc.tile_pool(name="keep", bufs=1))
        psum = ctx.enter_context(tc.psum_pool(name="psum", bufs=BANKS))

        def mx_tiles(name, width):
            codes = keep.tile([P, width], U32, name=name + "_codes", align_bytes=64)
            scales = keep.tile([P, width], U8, name=name + "_scales", align_bytes=64)
            return codes, scales

        offsets = keep.tile([P, S // LIST_ROWS], U16, name="offsets")
        x_rows = xT.rearrange("(p j) c -> p j c", j=PACK)
        x_raw = {}
        for u in range(2):
            for i, width in enumerate(X_LOADS[u]):
                start = sum(X_LOADS[u][:i])
                x_raw[u, i] = keep.tile([P, 2, width], F32, name="x_raw_%d_%d" % (u, i))
                nc.sync.dma_start(out=x_raw[u, i][:], in_=x_rows[:, 2 * u : 2 * u + 2, start : start + width])
            if u == 0:
                nc.sync.dma_start(offsets[:], offs)

        w1_rows = w1.rearrange("(p j) c -> p j c", j=PACK)
        w1_raw = []
        for h, width in enumerate(W1_LOADS):
            start = PACK * sum(W1_LOADS[:h])
            part = keep.tile([P, PACK, PACK * width], F32, name="w1_raw_%d" % h, align_bytes=64)
            nc.sync.dma_start(out=part[:], in_=w1_rows[:, :, start : start + PACK * width])
            w1_raw.append(part)
        w2_raw = keep.tile([P, PACK, N], F32, name="w2_raw")
        nc.sync.dma_start(out=w2_raw[:], in_=w2.rearrange("(p j) c -> p j c", j=PACK))

        windows = [keep.tile([P, T], U32, name="window_%d" % u) for u in range(2)]
        x_mx = [mx_tiles("x_%d" % g, GROUP) for g in range(S // GROUP)]

        picked = {
            g: keep.tile([P, GROUP, 2], U32, name="picked_%d" % g, align_bytes=64)
            for g in (FIRST_EARLY, FIRST_LATE, SECOND_EARLY)
        }
        second_late_runs = keep.tile([P, 2, GROUP], U32, name="second_late_runs")

        half = PACK * P * PACK // 2
        shared = keep.tile([P, 2 * half], U32, name="shared", align_bytes=64)
        w1_woven = shared[:, GROUP : GROUP + half].bitcast(BF16).rearrange("p (t m j) -> p t m j", t=PACK, j=PACK)

        def gather(u, g):
            if g == FIRST_LATE:
                dst = shared[:, u * half : u * half + GROUP]
            elif g == SECOND_LATE:
                dst = second_late_runs[:, u, :]
            else:
                dst = picked[g][:, :, u]
            entries = offsets[:, g * GROUP // LIST_ROWS : (g + 1) * GROUP // LIST_ROWS]
            nc.vector.tensor_copy(out=dst, in_=windows[u][:].indirect(entries))

        def quantize_x(g):
            quantize(*x_mx[g], picked[g][:].rearrange("p n u -> p (n u)").bitcast(BF16))

        for u in range(2):
            for i, width in enumerate(X_LOADS[u]):
                start = sum(X_LOADS[u][:i])
                cut = X_ON_VECTOR[u][i]
                for on_vector, a, b in ((True, 0, cut), (False, cut, width)):
                    if a < b:
                        round_copy(
                            on_vector,
                            windows[u][:, start + a : start + b].bitcast(BF16).rearrange("p (n e) -> p n e", e=2),
                            x_raw[u, i][:, :, a:b].rearrange("p e n -> p n e"),
                        )
            if u == 0:
                for g in (SECOND_EARLY, FIRST_EARLY, SECOND_LATE, FIRST_LATE):
                    gather(0, g)

        gather(1, SECOND_EARLY)
        gather(1, FIRST_EARLY)
        quantize_x(SECOND_EARLY)
        quantize_x(FIRST_EARLY)
        gather(1, SECOND_LATE)

        w1_mx = [mx_tiles("w1_%d" % t, P) for t in range(PACK)]
        for h, width in enumerate(W1_LOADS):
            start = sum(W1_LOADS[:h])
            round_copy(
                False,
                w1_woven[:, :, start : start + width, :].rearrange("p t m j -> p m j t"),
                w1_raw[h][:].rearrange("p j (m t) -> p m j t", t=PACK),
            )
        for t in range(PACK):
            quantize(*w1_mx[t], w1_woven[:, t, :, :].rearrange("p m j -> p (m j)"))

        picked[SECOND_LATE] = keep.tile(
            [P, GROUP, 2], U32, name="picked_second_late", tag="w1_raw_%d" % (len(W1_LOADS) - 1), align_bytes=64
        )
        nc.scalar.copy(out=picked[SECOND_LATE][:], in_=second_late_runs[:].rearrange("p u n -> p n u"))
        gather(1, FIRST_LATE)
        quantize_x(SECOND_LATE)
        nc.vector.tensor_copy(
            out=picked[FIRST_LATE][:].bitcast(I32),
            in_=shared[:].bitcast(I32).rearrange("p (u n) -> p n u", u=2)[:, 0:GROUP, :],
        )
        quantize_x(FIRST_LATE)

        bank = {}
        early = [(c, side) for c in range(CHUNKS // 2) for side in (SECOND, FIRST)]
        late = [(c, side) for side in (SECOND, FIRST) for c in range(CHUNKS // 2, CHUNKS)]
        for c, side in early + late:
            entry = side * V + c * CHUNK
            codes, scales = x_mx[entry // GROUP]
            cols = slice(entry % GROUP, entry % GROUP + CHUNK)
            bank[c, side] = psum.tile([P, PACK, CHUNK], F32, name="hidden", tag="bank")
            for t in range(PACK):
                multiply(bank[c, side][:, t, :], w1_mx[t][0][:], w1_mx[t][1][:], codes[:, cols], scales[:, cols])

        w2_woven = keep.tile([P, N, PACK], BF16, name="w2_woven", align_bytes=64)
        w2_codes, w2_scales = mx_tiles("w2", N)
        for on_vector, a, b in ((False, 0, W2_ON_SCALAR), (True, W2_ON_SCALAR, N)):
            round_copy(
                on_vector,
                w2_woven[:, a:b, :].rearrange("p (c i) j -> p c j i", i=4),
                w2_raw[:, :, a:b].rearrange("p j (c i) -> p c j i", i=4),
            )
        quantize(w2_codes, w2_scales, w2_woven[:].rearrange("p c j -> p (c j)"))

        relu_second = [keep.tile([P, CHUNK, PACK], F32, name="relu_second_%d" % c) for c in range(CHUNKS)]
        diff = [keep.tile([P, CHUNK, PACK], BF16, name="diff_%d" % c) for c in range(CHUNKS)]
        z = [keep.tile([P, CHUNK, PACK], BF16, name="z_%d" % c, align_bytes=64) for c in range(CHUNKS)]
        for c in range(CHUNKS):
            nc.scalar.activation(
                out=relu_second[c][:], in_=bank[c, SECOND][:].rearrange("p t n -> p n t"), func=ACT.Relu
            )
        for c in range(CHUNKS):
            nc.vector.scalar_tensor_tensor(
                out=diff[c][:],
                in0=bank[c, FIRST][:].rearrange("p t n -> p n t"),
                scalar=0.0,
                in1=relu_second[c][:],
                op0=ALU.max,
                op1=ALU.subtract,
            )
        for c in range(CHUNKS):
            cut = CHUNK if c < CHUNKS - 1 else CHUNK // 2
            nc.scalar.activation(out=z[c][:, 0:cut, :], in_=diff[c][:, 0:cut, :], func=ACT.Abs)
            if cut < CHUNK:
                rest = diff[c][:, cut:CHUNK, :]
                nc.vector.scalar_tensor_tensor(
                    out=z[c][:, cut:CHUNK, :], in0=rest, scalar=-1.0, in1=rest, op0=ALU.mult, op1=ALU.max
                )

        out_rows = out.rearrange("(r p) v -> p r v", p=P)
        for c in range(CHUNKS):
            z_codes, z_scales = mx_tiles("z_%d" % c, CHUNK)
            quantize(z_codes, z_scales, z[c][:].rearrange("p n t -> p (n t)"))
            result = keep.tile([P, N // P, CHUNK], F32, name="result_%d" % c)
            if c < CHUNKS - 1:
                acc = psum.tile([P, N // P, CHUNK], F32, name="acc", tag="bank")
                for r in range(N // P):
                    rows = slice(r * P, (r + 1) * P)
                    multiply(acc[:, r, :], w2_codes[:, rows], w2_scales[:, rows], z_codes[:], z_scales[:])
                nc.scalar.activation(out=result[:], in_=acc[:], func=ACT.Copy)
            else:
                for r in range(N // P):
                    rows = slice(r * P, (r + 1) * P)
                    acc = psum.tile([P, CHUNK], F32, name="acc", tag="bank")
                    multiply(acc[:], w2_codes[:, rows], w2_scales[:, rows], z_codes[:], z_scales[:])
                    if r == 0:
                        nc.scalar.activation(out=result[:, r, :], in_=acc[:], func=ACT.Copy)
                    else:
                        nc.vector.tensor_copy(out=result[:, r, :], in_=acc[:])
            nc.sync.dma_start(out=out_rows[:, :, c * CHUNK : (c + 1) * CHUNK], in_=result[:])
